import numpy as np
import ml_dtypes


def mxq(x, axis, fmt="e4m3"):
    dtype, down = {"e4m3": (ml_dtypes.float8_e4m3fn, 7), "e5m2": (ml_dtypes.float8_e5m2, 14)}[fmt]
    v = np.moveaxis(np.asarray(x, np.float32).astype(ml_dtypes.bfloat16).astype(np.float64), axis, -1)
    blocks = v.reshape(v.shape[:-1] + (-1, 32))
    amax = np.abs(blocks).max(-1, keepdims=True)
    byte = np.maximum(np.where(amax > 0, np.frexp(amax)[1] - 1 + 127, 0) - down, 1)
    scale = np.exp2(byte - 127.0)
    codes = (blocks / scale).astype(np.float32).astype(dtype).astype(np.float64)
    return np.moveaxis((codes * scale).reshape(v.shape), -1, axis)


WIDE = False


def mx_kscale(k):
    if not WIDE:
        return np.ones(k)
    levels = np.array([30, -30])
    if k % 512:
        return np.exp2(np.random.permutation(np.resize(levels, k // 32))).repeat(32)
    a = np.empty((k // 512, 16))
    for p in range(k // 512):
        a[p, :8] = np.random.permutation(np.resize(levels, 8))
        for g in range(8):
            far = levels[np.abs(levels - a[p, g]) >= 10]
            a[p, g + 8] = far[np.random.randint(len(far))]
    return np.exp2(a.ravel()).repeat(32)


def f64(x):
    return np.asarray(x).astype(np.float64)


E2M1 = np.array([0.0, 0.5, 1.0, 1.5, 2.0, 3.0, 4.0, 6.0, -0.0, -0.5, -1.0, -1.5, -2.0, -3.0, -4.0, -6.0])


def pack_weight(w, fmt):
    k, n = w.shape
    w = f64(np.asarray(w, np.float32).astype(ml_dtypes.bfloat16)).reshape(k // 32, 32, n)
    amax = np.abs(w).max(1)
    if fmt == "e4m3":
        byte = np.frexp(amax)[1] - 1 + 127 - 7
    else:
        mant, ex = np.frexp(amax / 6.0)
        byte = np.where(mant > 0.5, ex, ex - 1) + 127
    byte = np.clip(np.where(amax > 0, byte, 1), 1, 254)
    scaled = (w * np.exp2(127.0 - byte)[:, None, :]).reshape(k, n).astype(np.float32)
    by_word = np.ascontiguousarray(scaled.reshape(k // 512, 128, 4, n).transpose(0, 1, 3, 2))
    if fmt == "e4m3":
        words = by_word.astype(ml_dtypes.float8_e4m3fn).view(np.uint8)
    else:
        c = by_word.astype(ml_dtypes.float4_e2m1fn).view(np.uint8) & 0xF
        words = (c[..., 0::2] | (c[..., 1::2] << 4)).reshape(k // 512, 128, 2 * n)
    return np.ascontiguousarray(words), np.ascontiguousarray(byte.astype(np.uint8).reshape(k // 512, 16, n))


def unpack_weight(words, scales, fmt):
    g, _, n = scales.shape
    words = np.ascontiguousarray(words).reshape(g, 128, n, -1)
    if fmt == "e4m3":
        vals = words.view(ml_dtypes.float8_e4m3fn).astype(np.float64)
    else:
        nib = np.empty((g, 128, n, 4), np.uint8)
        nib[..., 0::2] = words & 0xF
        nib[..., 1::2] = words >> 4
        vals = E2M1[nib]
    vals = vals * np.repeat(np.exp2(scales.astype(np.float64) - 127.0), 8, axis=1)[..., None]
    return vals.transpose(0, 1, 3, 2).reshape(g * 512, n)


H, D, T = 2048, 1024, 1024


def setup_inputs():
    n = np.random.standard_normal
    s = mx_kscale(H)[:, None]
    p_wg = pack_weight(n((H, D)) / np.sqrt(H) / s, "e2m1")
    p_wu = pack_weight(n((H, D)) / np.sqrt(H) / s, "e4m3")
    return {
        "g": n((H, T)).astype(np.float32),
        "u": n((H, T)).astype(np.float32),
        "dh": (np.exp(0.5 * n((1, T))) * n((H, T)) * s).astype(np.float32),
        "wg_words": p_wg[0],
        "wg_scales": p_wg[1],
        "wu_words": p_wu[0],
        "wu_scales": p_wu[1],
        "r": (n((1024, 1024))).astype(np.float32),
    }


def reference(g, u, dh, wg_words, wg_scales, wu_words, wu_scales, r):
    sg = 1.0 / (1.0 + np.exp(-f64(g)))
    dg_ = mxq(f64(dh) * f64(u) * sg * (1.0 + f64(g) * (1.0 - sg)), 0, "e5m2")
    du_ = mxq(f64(dh) * f64(g) * sg, 0, "e5m2")
    wg_ = unpack_weight(wg_words, wg_scales, "e2m1")
    wu_ = unpack_weight(wu_words, wu_scales, "e4m3")
    y = wg_.T @ dg_ + wu_.T @ du_
    return f64(r) + y

@@ -1,0 +1,238 @@
+from contextlib import ExitStack
+
+import concourse.mybir as mybir
+
+H, D, T = 2048, 1024, 1024
+FLOPS = 2 * 2 * H * D * T
+
+F32 = mybir.dt.float32
+BF16 = mybir.dt.bfloat16
+I32 = mybir.dt.int32
+U32 = mybir.dt.uint32
+U8 = mybir.dt.uint8
+E5M2 = mybir.dt.float8_e5m2_x4
+E4M3 = mybir.dt.float8_e4m3fn_x4
+E2M1 = mybir.dt.float4_e2m1fn_x4
+ALU = mybir.AluOpType
+ACT = mybir.ActivationFunctionType
+
+P = 128
+PACK = 4
+K_PASS = P * PACK
+PASSES = H // K_PASS
+N_TILE = 512
+HALVES = T // N_TILE
+M_TILES = D // P
+
+
+def tile_mix_glubwd_fm_res_kernel(tc, g, u, dh, wg_words, wg_scales, wu_words, wu_scales, r, out):
+    nc = tc.nc
+    units = [(0, 0, 256), (0, 256, 256)] + [(c, 0, N_TILE) for c in range(1, HALVES * PASSES)]
+    n_units = len(units)
+
+    with ExitStack() as ctx:
+        raw = ctx.enter_context(tc.tile_pool(name="raw", bufs=3))
+        actp = ctx.enter_context(tc.tile_pool(name="actp", bufs=3))
+        grp = ctx.enter_context(tc.tile_pool(name="grp", bufs=2))
+        codep = ctx.enter_context(tc.tile_pool(name="codep", bufs=4))
+        keep = ctx.enter_context(tc.tile_pool(name="keep", bufs=1))
+        psum = ctx.enter_context(tc.psum_pool(name="psum", bufs=1))
+        ctx.enter_context(tc.manual_schedule())
+
+        warm = keep.tile([P, 8], F32, name="warm")
+        nc.vector.memset(warm[:], 0.0)
+        nc.scalar.activation(out=warm[:, 0:1], in_=warm[:, 1:2], func=ACT.Silu)
+
+        wg_plane = keep.tile([P, PASSES, D], U8, name="wg_plane", align_bytes=64)
+        wu_plane = keep.tile([P, PASSES, D], U8, name="wu_plane", align_bytes=64)
+        for plane, scales in ((wu_plane, wu_scales), (wg_plane, wg_scales)):
+            nc.vector.memset(plane[:].bitcast(U32), 0)
+            rows = scales.rearrange("a (q s) n -> s q a n", s=4)
+            for s in range(4):
+                nc.gpsimd.dma_start(out=plane[s:P:32, :, :].bitcast(I32), in_=rows[s].bitcast(I32))
+
+        st = {}
+        wts = {}
+        codes = {}
+        banks = {}
+        res = {}
+
+        def view(x, n):
+            chunk, c0, w = units[n]
+            half, a = divmod(chunk, PASSES)
+            t0 = half * N_TILE + c0
+            return x[a * K_PASS : (a + 1) * K_PASS, t0 : t0 + w].rearrange("(p j) t -> p j t", j=PACK)
+
+        def load(n, name, x):
+            w = units[n][2]
+            t = raw.tile([P, PACK, w], F32, name=name, tag=name)
+            nc.sync.dma_start(out=t[:], in_=view(x, n))
+            st[n, name] = t
+
+        def load_unit(n):
+            load(n, "g", g)
+            load(n, "dh", dh)
+            load(n, "u", u)
+
+        def load_weights(a):
+            wu_t = keep.tile([P, D], U32, name="wu%d" % a, align_bytes=64)
+            nc.sync.dma_start(out=wu_t[:].bitcast(I32), in_=wu_words[a].rearrange("p n i -> p (n i)").bitcast(I32))
+            wg_t = keep.tile([P, 2 * D], U8, name="wg%d" % a, align_bytes=64)
+            nc.sync.dma_start(out=wg_t[:].bitcast(I32), in_=wg_words[a].bitcast(I32))
+            wts[a] = (wg_t, wu_t)
+
+        def load_res(half):
+            t = keep.tile([P, M_TILES, N_TILE], F32, name="res%d" % half)
+            nc.sync.dma_start(out=t[:], in_=r[:, half * N_TILE : (half + 1) * N_TILE].rearrange("(m p) t -> p m t", p=P))
+            res[half] = t
+
+        def activations(n):
+            w = units[n][2]
+            gt = st[n, "g"]
+            first = actp.tile([P, PACK, w], F32, name="first", tag="first")
+            mneg = actp.tile([P, PACK, w], F32, name="mneg", tag="mneg")
+            if n % 2 == 0:
+                nc.scalar.activation(out=first[:], in_=gt[:], func=ACT.Silu)
+                nc.scalar.activation(out=mneg[:], in_=gt[:], func=ACT.Silu, scale=-1.0)
+                nc.scalar.activation(out=gt[:], in_=gt[:], func=ACT.Sigmoid)
+                st[n, "silu"], st[n, "sig"] = first, gt
+            else:
+                nc.scalar.activation(out=first[:], in_=gt[:], func=ACT.Sigmoid)
+                nc.scalar.activation(out=mneg[:], in_=gt[:], func=ACT.Silu, scale=-1.0)
+                nc.scalar.activation(out=gt[:], in_=gt[:], func=ACT.Silu)
+                st[n, "silu"], st[n, "sig"] = gt, first
+            st[n, "mneg"] = mneg
+
+        def product(n, name, x, y):
+            w = units[n][2]
+            t = grp.tile([P, PACK * w], BF16, name=name, tag=name, align_bytes=64)
+            nc.vector.tensor_tensor(
+                out=t[:].rearrange("p (c i j) -> p c j i", i=2, j=PACK),
+                in0=x[:].rearrange("p j (c i) -> p c j i", i=2),
+                in1=y[:].rearrange("p j (c i) -> p c j i", i=2),
+                op=ALU.mult,
+            )
+            st[n, name] = t
+
+        def make_du(n):
+            product(n, "du", st[n, "dh"], st[n, "silu"])
+
+        def make_q(n):
+            ut = st[n, "u"]
+            nc.vector.scalar_tensor_tensor(out=ut[:], in0=st[n, "dh"][:], scalar=-1.0, in1=ut[:], op0=ALU.mult, op1=ALU.mult)
+
+        def make_e(n):
+            m = st[n, "mneg"]
+            nc.vector.scalar_tensor_tensor(out=m[:], in0=m[:], scalar=1.0, in1=st[n, "sig"][:], op0=ALU.subtract, op1=ALU.mult)
+
+        def make_dg(n):
+            product(n, "dg", st[n, "u"], st[n, "mneg"])
+
+        def quantize(n, name):
+            chunk, c0, w = units[n]
+            if c0 == 0:
+                cw = codep.tile([P, N_TILE], U32, name=name + "_codes", tag=name + "_codes", align_bytes=64)
+                cs = codep.tile([P, N_TILE], U8, name=name + "_scales", tag=name + "_scales", align_bytes=64)
+                codes[chunk, name] = (cw, cs)
+            cw, cs = codes[chunk, name]
+            nc.vector.quantize_mx(out=cw[:, c0 : c0 + w].bitcast(E5M2), scales=cs[:, c0 : c0 + w], in_=st[n, name][:])
+
+        def multiply(chunk, name):
+            half, a = divmod(chunk, PASSES)
+            cw, cs = codes[chunk, name]
+            wg_t, wu_t = wts[a]
+            first = a == 0 and name == "du"
+            last = a == PASSES - 1 and name == "dg"
+            for m in range(M_TILES):
+                if first:
+                    banks[half, m] = psum.tile([P, N_TILE], F32, name="bank%d" % m, tag="bank%d" % m)
+                cols = slice(m * P, (m + 1) * P)
+                if name == "du":
+                    lhs, lhs_scale = wu_t[:, cols].bitcast(E4M3), wu_plane[:, a, cols]
+                else:
+                    lhs, lhs_scale = wg_t[:, 2 * m * P : 2 * (m + 1) * P].bitcast(E2M1), wg_plane[:, a, cols]
+                nc.tensor.matmul_mx(
+                    out=banks[half, m][:], lhsT=lhs, lhsT_scale=lhs_scale, rhs=cw[:].bitcast(E5M2), rhs_scale=cs[:], start=first, stop=last
+                )
+
+        def add_residual(half, m):
+            t = res[half]
+            nc.vector.tensor_tensor(out=t[:, m, :], in0=banks[half, m][:], in1=t[:, m, :], op=ALU.add)
+
+        def store(half, m0, m1):
+            dst = out[m0 * P : m1 * P, half * N_TILE : (half + 1) * N_TILE].rearrange("(m p) t -> p m t", p=P)
+            nc.sync.dma_start(out=dst, in_=res[half][:, m0:m1, :])
+
+        def vector_step(n):
+            steps = [make_du, make_q, make_e] if n % 2 == 0 else [make_q, make_e, make_du]
+            steps[0](n)
+            if n > 0:
+                quantize(n - 1, "dg")
+            steps[1](n)
+            steps[2](n)
+            if n % 2 == 0:
+                quantize(n, "du")
+                make_dg(n)
+            else:
+                make_dg(n)
+                quantize(n, "du")
+
+        for n in range(3):
+            load_unit(n)
+        activations(0)
+        activations(1)
+
+        vector_step(0)
+        load_unit(3)
+        activations(2)
+        vector_step(1)
+        load_weights(0)
+        load_unit(4)
+        activations(3)
+        vector_step(2)
+        multiply(0, "du")
+        multiply(0, "dg")
+        load_weights(1)
+        load_weights(2)
+        load_unit(5)
+        activations(4)
+        multiply(1, "du")
+        vector_step(3)
+        multiply(1, "dg")
+        multiply(2, "du")
+        load_weights(3)
+        load_unit(6)
+        activations(5)
+        vector_step(4)
+        multiply(2, "dg")
+        multiply(3, "du")
+        load(7, "g", g)
+        load_res(0)
+        load(7, "dh", dh)
+        load(7, "u", u)
+        activations(6)
+        vector_step(5)
+        multiply(3, "dg")
+        load_unit(8)
+        activations(7)
+        vector_step(6)
+        activations(8)
+        for m in range(M_TILES):
+            add_residual(0, m)
+        store(0, 0, 4)
+        store(0, 4, 8)
+        load_res(1)
+        multiply(4, "du")
+        multiply(4, "dg")
+        multiply(5, "du")
+        vector_step(7)
+        multiply(5, "dg")
+        multiply(6, "du")
+        vector_step(8)
+        multiply(6, "dg")
+        multiply(7, "du")
+        quantize(8, "dg")
+        multiply(7, "dg")
+        for m in range(M_TILES):
+            add_residual(1, m)
+            store(1, m, m + 1)

@@ -23,16 +23,24 @@ PASSES = H // K_PASS
 N_TILE = 512
 HALVES = T // N_TILE
 M_TILES = D // P
+EPILOGUE_STEP = 6
+TAIL_PIECE = 128
 
 
 def tile_mix_glubwd_fm_res_kernel(tc, g, u, dh, wg_words, wg_scales, wu_words, wu_scales, r, out):
     nc = tc.nc
-    units = [(0, 0, 256), (0, 256, 256)] + [(c, 0, N_TILE) for c in range(1, HALVES * PASSES)]
+    last_chunk = HALVES * PASSES - 1
+    units = []
+    for c in range(last_chunk + 1):
+        if c == 0:
+            units.extend([(c, 0, N_TILE // 2), (c, N_TILE // 2, N_TILE // 2)])
+        else:
+            units.append((c, 0, N_TILE))
     n_units = len(units)
 
     with ExitStack() as ctx:
         raw = ctx.enter_context(tc.tile_pool(name="raw", bufs=3))
-        actp = ctx.enter_context(tc.tile_pool(name="actp", bufs=3))
+        actp = ctx.enter_context(tc.tile_pool(name="actp", bufs=2))
         grp = ctx.enter_context(tc.tile_pool(name="grp", bufs=2))
         codep = ctx.enter_context(tc.tile_pool(name="codep", bufs=4))
         keep = ctx.enter_context(tc.tile_pool(name="keep", bufs=1))
@@ -65,7 +73,7 @@ def tile_mix_glubwd_fm_res_kernel(tc, g, u, dh, wg_words, wg_scales, wu_words, w
 
         def load(n, name, x):
             w = units[n][2]
-            t = raw.tile([P, PACK, w], F32, name=name, tag=name)
+            t = raw.tile([P, PACK, w], F32, name=name, tag=name, bufs=4 if name == "g" else 3)
             nc.sync.dma_start(out=t[:], in_=view(x, n))
             st[n, name] = t
 
@@ -86,56 +94,55 @@ def tile_mix_glubwd_fm_res_kernel(tc, g, u, dh, wg_words, wg_scales, wu_words, w
             nc.sync.dma_start(out=t[:], in_=r[:, half * N_TILE : (half + 1) * N_TILE].rearrange("(m p) t -> p m t", p=P))
             res[half] = t
 
-        def activations(n):
-            w = units[n][2]
-            gt = st[n, "g"]
-            first = actp.tile([P, PACK, w], F32, name="first", tag="first")
-            mneg = actp.tile([P, PACK, w], F32, name="mneg", tag="mneg")
-            if n % 2 == 0:
-                nc.scalar.activation(out=first[:], in_=gt[:], func=ACT.Silu)
-                nc.scalar.activation(out=mneg[:], in_=gt[:], func=ACT.Silu, scale=-1.0)
-                nc.scalar.activation(out=gt[:], in_=gt[:], func=ACT.Sigmoid)
-                st[n, "silu"], st[n, "sig"] = first, gt
-            else:
-                nc.scalar.activation(out=first[:], in_=gt[:], func=ACT.Sigmoid)
-                nc.scalar.activation(out=mneg[:], in_=gt[:], func=ACT.Silu, scale=-1.0)
-                nc.scalar.activation(out=gt[:], in_=gt[:], func=ACT.Silu)
-                st[n, "silu"], st[n, "sig"] = gt, first
-            st[n, "mneg"] = mneg
-
-        def product(n, name, x, y):
-            w = units[n][2]
-            t = grp.tile([P, PACK * w], BF16, name=name, tag=name, align_bytes=64)
-            nc.vector.tensor_tensor(
-                out=t[:].rearrange("p (c i j) -> p c j i", i=2, j=PACK),
-                in0=x[:].rearrange("p j (c i) -> p c j i", i=2),
-                in1=y[:].rearrange("p j (c i) -> p c j i", i=2),
-                op=ALU.mult,
-            )
+        def activate(n, name, func, scale):
+            t = actp.tile([P, PACK, units[n][2]], F32, name=name, tag=name)
+            nc.scalar.activation(out=t[:], in_=st[n, "g"][:], func=func, scale=scale)
             st[n, name] = t
 
-        def make_du(n):
-            product(n, "du", st[n, "dh"], st[n, "silu"])
+        def make_th(n):
+            activate(n, "th", ACT.Tanh, 0.5)
 
-        def make_q(n):
+        def make_mneg(n):
+            activate(n, "mneg", ACT.Silu, -1.0)
+
+        def make_p(n):
+            th = st[n, "th"]
+            nc.vector.scalar_tensor_tensor(out=th[:], in0=th[:], scalar=1.0, in1=st[n, "dh"][:], op0=ALU.add, op1=ALU.mult)
+
+        def make_w(n):
             ut = st[n, "u"]
-            nc.vector.scalar_tensor_tensor(out=ut[:], in0=st[n, "dh"][:], scalar=-1.0, in1=ut[:], op0=ALU.mult, op1=ALU.mult)
+            nc.vector.scalar_tensor_tensor(out=ut[:], in0=st[n, "mneg"][:], scalar=1.0, in1=ut[:], op0=ALU.subtract, op1=ALU.mult)
 
-        def make_e(n):
-            m = st[n, "mneg"]
-            nc.vector.scalar_tensor_tensor(out=m[:], in0=m[:], scalar=1.0, in1=st[n, "sig"][:], op0=ALU.subtract, op1=ALU.mult)
+        def make_du(n):
+            gt = st[n, "g"]
+            nc.vector.tensor_tensor(out=gt[:], in0=st[n, "th"][:], in1=gt[:], op=ALU.mult)
 
-        def make_dg(n):
-            product(n, "dg", st[n, "u"], st[n, "mneg"])
+        def make_dg(n, cols, dst):
+            nc.vector.tensor_tensor(out=dst[:], in0=st[n, "th"][:, :, cols], in1=st[n, "u"][:, :, cols], op=ALU.mult)
 
-        def quantize(n, name):
+        def interleave(name, src, pool, tag):
+            t = pool.tile([P, PACK * src.shape[2]], BF16, name=tag, tag=tag, align_bytes=64)
+            nc.scalar.activation(
+                out=t[:].rearrange("p (c i j) -> p c j i", i=2, j=PACK),
+                in_=src[:].rearrange("p j (c i) -> p c j i", i=2),
+                func=ACT.Copy,
+                scale=0.5 if name == "du" else -0.5,
+            )
+            return t
+
+        def quantize(n, name, cols, src):
             chunk, c0, w = units[n]
-            if c0 == 0:
+            if c0 + cols.start == 0:
                 cw = codep.tile([P, N_TILE], U32, name=name + "_codes", tag=name + "_codes", align_bytes=64)
                 cs = codep.tile([P, N_TILE], U8, name=name + "_scales", tag=name + "_scales", align_bytes=64)
                 codes[chunk, name] = (cw, cs)
             cw, cs = codes[chunk, name]
-            nc.vector.quantize_mx(out=cw[:, c0 : c0 + w].bitcast(E5M2), scales=cs[:, c0 : c0 + w], in_=st[n, name][:])
+            words = slice(c0 + cols.start, c0 + cols.stop)
+            nc.vector.quantize_mx(
+                out=cw[:, words].bitcast(E5M2), scales=cs[:, words], in_=src[:]
+            )
+            if words.stop == N_TILE:
+                ready.append((chunk, name))
 
         def multiply(chunk, name):
             half, a = divmod(chunk, PASSES)
@@ -163,76 +170,69 @@ def tile_mix_glubwd_fm_res_kernel(tc, g, u, dh, wg_words, wg_scales, wu_words, w
             dst = out[m0 * P : m1 * P, half * N_TILE : (half + 1) * N_TILE].rearrange("(m p) t -> p m t", p=P)
             nc.sync.dma_start(out=dst, in_=res[half][:, m0:m1, :])
 
-        def vector_step(n):
-            steps = [make_du, make_q, make_e] if n % 2 == 0 else [make_q, make_e, make_du]
-            steps[0](n)
-            if n > 0:
-                quantize(n - 1, "dg")
-            steps[1](n)
-            steps[2](n)
-            if n % 2 == 0:
-                quantize(n, "du")
-                make_dg(n)
-            else:
-                make_dg(n)
-                quantize(n, "du")
+        def multiply_ready(limit):
+            while ready and ready[0][0] < limit:
+                multiply(*ready[0])
+                ready.remove(ready[0])
 
+        def whole(n):
+            return slice(0, units[n][2])
+
+        ready = []
+        last = n_units - 1
         for n in range(3):
             load_unit(n)
-        activations(0)
-        activations(1)
-
-        vector_step(0)
-        load_unit(3)
-        activations(2)
-        vector_step(1)
-        load_weights(0)
-        load_unit(4)
-        activations(3)
-        vector_step(2)
-        multiply(0, "du")
-        multiply(0, "dg")
-        load_weights(1)
-        load_weights(2)
-        load_unit(5)
-        activations(4)
-        multiply(1, "du")
-        vector_step(3)
-        multiply(1, "dg")
-        multiply(2, "du")
-        load_weights(3)
-        load_unit(6)
-        activations(5)
-        vector_step(4)
-        multiply(2, "dg")
-        multiply(3, "du")
-        load(7, "g", g)
-        load_res(0)
-        load(7, "dh", dh)
-        load(7, "u", u)
-        activations(6)
-        vector_step(5)
-        multiply(3, "dg")
-        load_unit(8)
-        activations(7)
-        vector_step(6)
-        activations(8)
-        for m in range(M_TILES):
-            add_residual(0, m)
-        store(0, 0, 4)
-        store(0, 4, 8)
-        load_res(1)
-        multiply(4, "du")
-        multiply(4, "dg")
-        multiply(5, "du")
-        vector_step(7)
-        multiply(5, "dg")
-        multiply(6, "du")
-        vector_step(8)
-        multiply(6, "dg")
-        multiply(7, "du")
-        quantize(8, "dg")
-        multiply(7, "dg")
+        make_th(0)
+        make_mneg(0)
+        for n in range(n_units):
+            make_p(n)
+            if n > 0:
+                quantize(n - 1, "du", whole(n - 1), st[n - 1, "du"])
+            if n < last:
+                make_th(n + 1)
+            else:
+                quantize(n - 1, "dg", whole(n - 1), st[n - 1, "dg"])
+                multiply_ready(last_chunk + 1)
+            make_du(n)
+            st[n, "du"] = interleave("du", st[n, "g"], grp, "du")
+            if n < last:
+                make_mneg(n + 1)
+            make_w(n)
+            if n == last:
+                break
+            if n > 0:
+                quantize(n - 1, "dg", whole(n - 1), st[n - 1, "dg"])
+            if n >= 2:
+                multiply_ready(PASSES if n <= EPILOGUE_STEP else last_chunk + 1)
+            make_dg(n, whole(n), st[n, "mneg"])
+            st[n, "dg"] = interleave("dg", st[n, "mneg"], grp, "dg")
+            if n == EPILOGUE_STEP:
+                for m in range(M_TILES):
+                    add_residual(0, m)
+                multiply_ready(last_chunk + 1)
+            if 1 <= n <= PASSES:
+                load_weights(n - 1)
+            if n + 3 < n_units:
+                load(n + 3, "g", g)
+                if n == 4:
+                    load_res(0)
+                load(n + 3, "dh", dh)
+                load(n + 3, "u", u)
+            if n == EPILOGUE_STEP:
+                store(0, 0, 4)
+                store(0, 4, 8)
+                load_res(1)
+        pieces = [slice(c, c + TAIL_PIECE) for c in range(0, N_TILE, TAIL_PIECE)]
+        quantize(last, "du", whole(last), st[last, "du"])
+        multiply_ready(last_chunk + 1)
+        grouped = []
+        for i, cols in enumerate(pieces):
+            piece = keep.tile([P, PACK, TAIL_PIECE], F32, name="piece%d" % i)
+            make_dg(last, cols, piece)
+            grouped.append(interleave("dg", piece, keep, "piece_bf%d" % i))
+        for cols, src in zip(pieces, grouped):
+            quantize(last, "dg", cols, src)
+        multiply_ready(last_chunk + 1)
         for m in range(M_TILES):
             add_residual(1, m)
             store(1, m, m + 1)

@@ -23,23 +23,23 @@ PASSES = H // K_PASS
 N_TILE = 512
 HALVES = T // N_TILE
 M_TILES = D // P
-EPILOGUE_STEP = 6
+EPILOGUE_CHUNK = 5
+SLOTS_PER_UNIT = {0: 1, 1: 2}
+WEIGHTS_AFTER = {0: (0,), 1: (1, 2), 2: (3,)}
 TAIL_PIECE = 128
 
 
 def tile_mix_glubwd_fm_res_kernel(tc, g, u, dh, wg_words, wg_scales, wu_words, wu_scales, r, out):
     nc = tc.nc
-    last_chunk = HALVES * PASSES - 1
+    n_chunks = HALVES * PASSES
     units = []
-    for c in range(last_chunk + 1):
-        if c == 0:
-            units.extend([(c, 0, N_TILE // 2), (c, N_TILE // 2, N_TILE // 2)])
-        else:
-            units.append((c, 0, N_TILE))
-    n_units = len(units)
+    for c in range(n_chunks):
+        step = SLOTS_PER_UNIT.get(c, PACK)
+        units.extend([(c, j, j + step) for j in range(0, PACK, step)])
+    last = len(units) - 1
 
     with ExitStack() as ctx:
-        raw = ctx.enter_context(tc.tile_pool(name="raw", bufs=3))
+        raw = ctx.enter_context(tc.tile_pool(name="raw", bufs=4))
         actp = ctx.enter_context(tc.tile_pool(name="actp", bufs=2))
         grp = ctx.enter_context(tc.tile_pool(name="grp", bufs=2))
         codep = ctx.enter_context(tc.tile_pool(name="codep", bufs=4))
@@ -59,28 +59,18 @@ def tile_mix_glubwd_fm_res_kernel(tc, g, u, dh, wg_words, wg_scales, wu_words, w
             for s in range(4):
                 nc.gpsimd.dma_start(out=plane[s:P:32, :, :].bitcast(I32), in_=rows[s].bitcast(I32))
 
-        st = {}
-        wts = {}
-        codes = {}
-        banks = {}
-        res = {}
+        srcs = {"g": g, "dh": dh, "u": u}
+        rawt, st, wts, codes, banks, res, bf = {}, {}, {}, {}, {}, {}, {}
 
-        def view(x, n):
-            chunk, c0, w = units[n]
-            half, a = divmod(chunk, PASSES)
-            t0 = half * N_TILE + c0
-            return x[a * K_PASS : (a + 1) * K_PASS, t0 : t0 + w].rearrange("(p j) t -> p j t", j=PACK)
-
-        def load(n, name, x):
-            w = units[n][2]
-            t = raw.tile([P, PACK, w], F32, name=name, tag=name, bufs=4 if name == "g" else 3)
-            nc.sync.dma_start(out=t[:], in_=view(x, n))
-            st[n, name] = t
-
-        def load_unit(n):
-            load(n, "g", g)
-            load(n, "dh", dh)
-            load(n, "u", u)
+        def load_chunk(c):
+            half, a = divmod(c, PASSES)
+            for name in srcs:
+                rawt[c, name] = raw.tile([P, PACK, N_TILE], F32, name=name, tag=name, bufs=3 if name == "dh" else 4)
+            for cc, j0, j1 in units:
+                if cc == c:
+                    for name in srcs:
+                        rows = srcs[name][a * K_PASS : (a + 1) * K_PASS, half * N_TILE : (half + 1) * N_TILE]
+                        nc.sync.dma_start(out=rawt[c, name][:, j0:j1, :], in_=rows.rearrange("(p j) t -> p j t", j=PACK)[:, j0:j1, :])
 
         def load_weights(a):
             wu_t = keep.tile([P, D], U32, name="wu%d" % a, align_bytes=64)
@@ -90,149 +80,161 @@ def tile_mix_glubwd_fm_res_kernel(tc, g, u, dh, wg_words, wg_scales, wu_words, w
             wts[a] = (wg_t, wu_t)
 
         def load_res(half):
-            t = keep.tile([P, M_TILES, N_TILE], F32, name="res%d" % half)
-            nc.sync.dma_start(out=t[:], in_=r[:, half * N_TILE : (half + 1) * N_TILE].rearrange("(m p) t -> p m t", p=P))
-            res[half] = t
+            res[half] = keep.tile([P, M_TILES, N_TILE], F32, name="res%d" % half)
+            nc.sync.dma_start(out=res[half][:], in_=r[:, half * N_TILE : (half + 1) * N_TILE].rearrange("(m p) t -> p m t", p=P))
 
-        def activate(n, name, func, scale):
-            t = actp.tile([P, PACK, units[n][2]], F32, name=name, tag=name)
-            nc.scalar.activation(out=t[:], in_=st[n, "g"][:], func=func, scale=scale)
-            st[n, name] = t
+        def part(n, name):
+            c, j0, j1 = units[n]
+            return rawt[c, name][:, j0:j1, :]
+
+        def scratch(n, name):
+            c, j0, j1 = units[n]
+            st[n, name] = actp.tile([P, j1 - j0, N_TILE], F32, name=name, tag=name)
+            return st[n, name][:]
 
         def make_th(n):
-            activate(n, "th", ACT.Tanh, 0.5)
+            nc.scalar.activation(out=scratch(n, "th"), in_=part(n, "g"), func=ACT.Tanh, scale=0.5)
 
         def make_mneg(n):
-            activate(n, "mneg", ACT.Silu, -1.0)
+            nc.scalar.activation(out=scratch(n, "mneg"), in_=part(n, "g"), func=ACT.Silu, scale=-1.0)
 
         def make_p(n):
-            th = st[n, "th"]
-            nc.vector.scalar_tensor_tensor(out=th[:], in0=th[:], scalar=1.0, in1=st[n, "dh"][:], op0=ALU.add, op1=ALU.mult)
-
-        def make_w(n):
-            ut = st[n, "u"]
-            nc.vector.scalar_tensor_tensor(out=ut[:], in0=st[n, "mneg"][:], scalar=1.0, in1=ut[:], op0=ALU.subtract, op1=ALU.mult)
+            th = st[n, "th"][:]
+            nc.vector.scalar_tensor_tensor(out=th, in0=th, scalar=1.0, in1=part(n, "dh"), op0=ALU.add, op1=ALU.mult)
 
         def make_du(n):
-            gt = st[n, "g"]
-            nc.vector.tensor_tensor(out=gt[:], in0=st[n, "th"][:], in1=gt[:], op=ALU.mult)
+            nc.vector.tensor_tensor(out=part(n, "g"), in0=st[n, "th"][:], in1=part(n, "g"), op=ALU.mult)
 
-        def make_dg(n, cols, dst):
-            nc.vector.tensor_tensor(out=dst[:], in0=st[n, "th"][:, :, cols], in1=st[n, "u"][:, :, cols], op=ALU.mult)
+        def make_w(n):
+            m = st[n, "mneg"][:]
+            nc.vector.scalar_tensor_tensor(out=m, in0=m, scalar=1.0, in1=part(n, "u"), op0=ALU.subtract, op1=ALU.mult)
 
-        def interleave(name, src, pool, tag):
-            t = pool.tile([P, PACK * src.shape[2]], BF16, name=tag, tag=tag, align_bytes=64)
+        def make_dg(n):
+            nc.vector.tensor_tensor(out=part(n, "u"), in0=st[n, "th"][:], in1=st[n, "mneg"][:], op=ALU.mult)
+
+        def round_interleave(name, src, dst):
             nc.scalar.activation(
-                out=t[:].rearrange("p (c i j) -> p c j i", i=2, j=PACK),
-                in_=src[:].rearrange("p j (c i) -> p c j i", i=2),
+                out=dst.rearrange("p (c i j) -> p c j i", i=2, j=PACK),
+                in_=src.rearrange("p j (c i) -> p c j i", i=2),
                 func=ACT.Copy,
                 scale=0.5 if name == "du" else -0.5,
             )
-            return t
 
-        def quantize(n, name, cols, src):
-            chunk, c0, w = units[n]
-            if c0 + cols.start == 0:
-                cw = codep.tile([P, N_TILE], U32, name=name + "_codes", tag=name + "_codes", align_bytes=64)
-                cs = codep.tile([P, N_TILE], U8, name=name + "_scales", tag=name + "_scales", align_bytes=64)
-                codes[chunk, name] = (cw, cs)
-            cw, cs = codes[chunk, name]
-            words = slice(c0 + cols.start, c0 + cols.stop)
-            nc.vector.quantize_mx(
-                out=cw[:, words].bitcast(E5M2), scales=cs[:, words], in_=src[:]
-            )
-            if words.stop == N_TILE:
-                ready.append((chunk, name))
+        def copy_du(c):
+            bf[c] = grp.tile([P, 2 * PACK * N_TILE], BF16, name="bf", tag="bf", align_bytes=64)
+            round_interleave("du", rawt[c, "g"][:], bf[c][:, : PACK * N_TILE])
 
-        def multiply(chunk, name):
-            half, a = divmod(chunk, PASSES)
-            cw, cs = codes[chunk, name]
+        def copy_dg(c):
+            round_interleave("dg", rawt[c, "u"][:], bf[c][:, PACK * N_TILE :])
+
+        def quantize(c, first, src):
+            if first == 0:
+                cw = codep.tile([P, 2 * N_TILE], U32, name="codes", tag="codes", align_bytes=64)
+                cs = codep.tile([P, 2 * N_TILE], U8, name="scales", tag="scales", align_bytes=64)
+                codes[c] = (cw, cs)
+            cw, cs = codes[c]
+            cols = slice(first, first + src.shape[1] // PACK)
+            nc.vector.quantize_mx(out=cw[:, cols].bitcast(E5M2), scales=cs[:, cols], in_=src)
+
+        def multiply(c, name, m):
+            half, a = divmod(c, PASSES)
+            cw, cs = codes[c]
+            words = slice(0, N_TILE) if name == "du" else slice(N_TILE, 2 * N_TILE)
             wg_t, wu_t = wts[a]
             first = a == 0 and name == "du"
-            last = a == PASSES - 1 and name == "dg"
-            for m in range(M_TILES):
-                if first:
-                    banks[half, m] = psum.tile([P, N_TILE], F32, name="bank%d" % m, tag="bank%d" % m)
-                cols = slice(m * P, (m + 1) * P)
-                if name == "du":
-                    lhs, lhs_scale = wu_t[:, cols].bitcast(E4M3), wu_plane[:, a, cols]
-                else:
-                    lhs, lhs_scale = wg_t[:, 2 * m * P : 2 * (m + 1) * P].bitcast(E2M1), wg_plane[:, a, cols]
-                nc.tensor.matmul_mx(
-                    out=banks[half, m][:], lhsT=lhs, lhsT_scale=lhs_scale, rhs=cw[:].bitcast(E5M2), rhs_scale=cs[:], start=first, stop=last
-                )
+            if first:
+                banks[half, m] = psum.tile([P, N_TILE], F32, name="bank%d" % m, tag="bank%d" % m)
+            cols = slice(m * P, (m + 1) * P)
+            if name == "du":
+                lhs, lhs_scale = wu_t[:, cols].bitcast(E4M3), wu_plane[:, a, cols]
+            else:
+                lhs, lhs_scale = wg_t[:, 2 * m * P : 2 * (m + 1) * P].bitcast(E2M1), wg_plane[:, a, cols]
+            nc.tensor.matmul_mx(
+                out=banks[half, m][:], lhsT=lhs, lhsT_scale=lhs_scale, rhs=cw[:, words].bitcast(E5M2), rhs_scale=cs[:, words],
+                start=first, stop=(a == PASSES - 1 and name == "dg"),
+            )
+
+        def multiply_all(c, names):
+            for name in names:
+                for m in range(M_TILES):
+                    multiply(c, name, m)
 
         def add_residual(half, m):
-            t = res[half]
-            nc.vector.tensor_tensor(out=t[:, m, :], in0=banks[half, m][:], in1=t[:, m, :], op=ALU.add)
+            t = res[half][:, m, :]
+            nc.vector.tensor_tensor(out=t, in0=banks[half, m][:], in1=t, op=ALU.add)
 
         def store(half, m0, m1):
             dst = out[m0 * P : m1 * P, half * N_TILE : (half + 1) * N_TILE].rearrange("(m p) t -> p m t", p=P)
             nc.sync.dma_start(out=dst, in_=res[half][:, m0:m1, :])
 
-        def multiply_ready(limit):
-            while ready and ready[0][0] < limit:
-                multiply(*ready[0])
-                ready.remove(ready[0])
-
-        def whole(n):
-            return slice(0, units[n][2])
-
-        ready = []
-        last = n_units - 1
-        for n in range(3):
-            load_unit(n)
+        both = ("du", "dg")
+        for c in range(3):
+            load_chunk(c)
         make_th(0)
         make_mneg(0)
-        for n in range(n_units):
+        for n in range(last):
+            c, j0, j1 = units[n]
+            if c == 2:
+                quantize(0, 0, bf[0][:])
+                multiply_all(0, both)
             make_p(n)
-            if n > 0:
-                quantize(n - 1, "du", whole(n - 1), st[n - 1, "du"])
-            if n < last:
-                make_th(n + 1)
-            else:
-                quantize(n - 1, "dg", whole(n - 1), st[n - 1, "dg"])
-                multiply_ready(last_chunk + 1)
-            make_du(n)
-            st[n, "du"] = interleave("du", st[n, "g"], grp, "du")
-            if n < last:
-                make_mneg(n + 1)
+            make_th(n + 1)
             make_w(n)
-            if n == last:
-                break
-            if n > 0:
-                quantize(n - 1, "dg", whole(n - 1), st[n - 1, "dg"])
-            if n >= 2:
-                multiply_ready(PASSES if n <= EPILOGUE_STEP else last_chunk + 1)
-            make_dg(n, whole(n), st[n, "mneg"])
-            st[n, "dg"] = interleave("dg", st[n, "mneg"], grp, "dg")
-            if n == EPILOGUE_STEP:
+            make_mneg(n + 1)
+            if c == 1 and j0 == 0:
+                copy_du(0)
+                copy_dg(0)
+            make_du(n)
+            if c > 1:
+                quantize(c - 1, 0, bf[c - 1][:])
+            if j1 == PACK and c > 0:
+                copy_du(c)
+            make_dg(n)
+            if j1 < PACK:
+                continue
+            if c > 0:
+                copy_dg(c)
+            for a in WEIGHTS_AFTER.get(c, ()):
+                load_weights(a)
+            if 2 <= c <= PASSES:
+                multiply_all(c - 1, both)
+            if c == EPILOGUE_CHUNK:
                 for m in range(M_TILES):
                     add_residual(0, m)
-                multiply_ready(last_chunk + 1)
-            if 1 <= n <= PASSES:
-                load_weights(n - 1)
-            if n + 3 < n_units:
-                load(n + 3, "g", g)
-                if n == 4:
-                    load_res(0)
-                load(n + 3, "dh", dh)
-                load(n + 3, "u", u)
-            if n == EPILOGUE_STEP:
+                multiply_all(PASSES, both)
+            if c > EPILOGUE_CHUNK:
+                multiply_all(c - 1, both)
+            if c == 3:
+                load_res(0)
+            if c + 3 < n_chunks:
+                load_chunk(c + 3)
+            if c == EPILOGUE_CHUNK:
                 store(0, 0, 4)
                 store(0, 4, 8)
                 load_res(1)
-        pieces = [slice(c, c + TAIL_PIECE) for c in range(0, N_TILE, TAIL_PIECE)]
-        quantize(last, "du", whole(last), st[last, "du"])
-        multiply_ready(last_chunk + 1)
-        grouped = []
-        for i, cols in enumerate(pieces):
+
+        c = n_chunks - 1
+        make_p(last)
+        quantize(c - 1, 0, bf[c - 1][:, : PACK * N_TILE])
+        multiply_all(c - 1, ("du",))
+        make_du(last)
+        copy_du(c)
+        quantize(c - 1, N_TILE, bf[c - 1][:, PACK * N_TILE :])
+        multiply_all(c - 1, ("dg",))
+        make_w(last)
+        quantize(c, 0, bf[c][:, : PACK * N_TILE])
+        multiply_all(c, ("du",))
+        pieces = []
+        for i in range(N_TILE // TAIL_PIECE):
+            cols = slice(i * TAIL_PIECE, (i + 1) * TAIL_PIECE)
             piece = keep.tile([P, PACK, TAIL_PIECE], F32, name="piece%d" % i)
-            make_dg(last, cols, piece)
-            grouped.append(interleave("dg", piece, keep, "piece_bf%d" % i))
-        for cols, src in zip(pieces, grouped):
-            quantize(last, "dg", cols, src)
-        multiply_ready(last_chunk + 1)
+            nc.vector.tensor_tensor(out=piece[:], in0=st[last, "th"][:, :, cols], in1=st[last, "mneg"][:, :, cols], op=ALU.mult)
+            piece_bf = keep.tile([P, PACK * TAIL_PIECE], BF16, name="piece_bf%d" % i, align_bytes=64)
+            round_interleave("dg", piece[:], piece_bf[:])
+            pieces.append(piece_bf)
+        for i, piece_bf in enumerate(pieces):
+            quantize(c, N_TILE + i * TAIL_PIECE, piece_bf[:])
+        multiply_all(c, ("dg",))
         for m in range(M_TILES):
             add_residual(1, m)
             store(1, m, m + 1)

@@ -23,7 +23,7 @@ PASSES = H // K_PASS
 N_TILE = 512
 HALVES = T // N_TILE
 M_TILES = D // P
-EPILOGUE_CHUNK = 5
+EPILOGUE_CHUNK = 6
 SLOTS_PER_UNIT = {0: 1, 1: 2}
 WEIGHTS_AFTER = {0: (0,), 1: (1, 2), 2: (3,)}
 TAIL_PIECE = 128
@@ -47,10 +47,6 @@ def tile_mix_glubwd_fm_res_kernel(tc, g, u, dh, wg_words, wg_scales, wu_words, w
         psum = ctx.enter_context(tc.psum_pool(name="psum", bufs=1))
         ctx.enter_context(tc.manual_schedule())
 
-        warm = keep.tile([P, 8], F32, name="warm")
-        nc.vector.memset(warm[:], 0.0)
-        nc.scalar.activation(out=warm[:, 0:1], in_=warm[:, 1:2], func=ACT.Silu)
-
         wg_plane = keep.tile([P, PASSES, D], U8, name="wg_plane", align_bytes=64)
         wu_plane = keep.tile([P, PASSES, D], U8, name="wu_plane", align_bytes=64)
         for plane, scales in ((wu_plane, wu_scales), (wg_plane, wg_scales)):
@@ -69,6 +65,8 @@ def tile_mix_glubwd_fm_res_kernel(tc, g, u, dh, wg_words, wg_scales, wu_words, w
             for cc, j0, j1 in units:
                 if cc == c:
                     for name in srcs:
+                        if c == EPILOGUE_CHUNK and name == "u":
+                            load_res(0)
                         rows = srcs[name][a * K_PASS : (a + 1) * K_PASS, half * N_TILE : (half + 1) * N_TILE]
                         nc.sync.dma_start(out=rawt[c, name][:, j0:j1, :], in_=rows.rearrange("(p j) t -> p j t", j=PACK)[:, j0:j1, :])
 
@@ -102,8 +100,8 @@ def tile_mix_glubwd_fm_res_kernel(tc, g, u, dh, wg_words, wg_scales, wu_words, w
             th = st[n, "th"][:]
             nc.vector.scalar_tensor_tensor(out=th, in0=th, scalar=1.0, in1=part(n, "dh"), op0=ALU.add, op1=ALU.mult)
 
-        def make_du(n):
-            nc.vector.tensor_tensor(out=part(n, "g"), in0=st[n, "th"][:], in1=part(n, "g"), op=ALU.mult)
+        def make_du(n, engine):
+            engine.tensor_tensor(out=part(n, "g"), in0=st[n, "th"][:], in1=part(n, "g"), op=ALU.mult)
 
         def make_w(n):
             m = st[n, "mneg"][:]
@@ -170,8 +168,8 @@ def tile_mix_glubwd_fm_res_kernel(tc, g, u, dh, wg_words, wg_scales, wu_words, w
         both = ("du", "dg")
         for c in range(3):
             load_chunk(c)
-        make_th(0)
         make_mneg(0)
+        make_th(0)
         for n in range(last):
             c, j0, j1 = units[n]
             if c == 2:
@@ -179,12 +177,20 @@ def tile_mix_glubwd_fm_res_kernel(tc, g, u, dh, wg_words, wg_scales, wu_words, w
                 multiply_all(0, both)
             make_p(n)
             make_th(n + 1)
+            if c == EPILOGUE_CHUNK:
+                make_du(n, nc.gpsimd)
+                for m in range(M_TILES):
+                    add_residual(0, m)
+                multiply_all(PASSES, both)
+                store(0, 0, 4)
+                store(0, 4, 8)
             make_w(n)
             make_mneg(n + 1)
             if c == 1 and j0 == 0:
                 copy_du(0)
                 copy_dg(0)
-            make_du(n)
+            if c != EPILOGUE_CHUNK:
+                make_du(n, nc.vector)
             if c > 1:
                 quantize(c - 1, 0, bf[c - 1][:])
             if j1 == PACK and c > 0:
@@ -199,25 +205,17 @@ def tile_mix_glubwd_fm_res_kernel(tc, g, u, dh, wg_words, wg_scales, wu_words, w
             if 2 <= c <= PASSES:
                 multiply_all(c - 1, both)
             if c == EPILOGUE_CHUNK:
-                for m in range(M_TILES):
-                    add_residual(0, m)
-                multiply_all(PASSES, both)
-            if c > EPILOGUE_CHUNK:
                 multiply_all(c - 1, both)
-            if c == 3:
-                load_res(0)
             if c + 3 < n_chunks:
                 load_chunk(c + 3)
-            if c == EPILOGUE_CHUNK:
-                store(0, 0, 4)
-                store(0, 4, 8)
+            if c + 3 == n_chunks - 1:
                 load_res(1)
 
         c = n_chunks - 1
         make_p(last)
         quantize(c - 1, 0, bf[c - 1][:, : PACK * N_TILE])
         multiply_all(c - 1, ("du",))
-        make_du(last)
+        make_du(last, nc.vector)
         copy_du(c)
         quantize(c - 1, N_TILE, bf[c - 1][:, PACK * N_TILE :])
         multiply_all(c - 1, ("dg",))

from contextlib import ExitStack

import concourse.mybir as mybir

H, D, T = 2048, 1024, 1024
FLOPS = 2 * 2 * H * D * T

F32 = mybir.dt.float32
BF16 = mybir.dt.bfloat16
I32 = mybir.dt.int32
U32 = mybir.dt.uint32
U8 = mybir.dt.uint8
E5M2 = mybir.dt.float8_e5m2_x4
E4M3 = mybir.dt.float8_e4m3fn_x4
E2M1 = mybir.dt.float4_e2m1fn_x4
ALU = mybir.AluOpType
ACT = mybir.ActivationFunctionType

P = 128
PACK = 4
K_PASS = P * PACK
PASSES = H // K_PASS
N_TILE = 512
HALVES = T // N_TILE
M_TILES = D // P
EPILOGUE_CHUNK = 6
SLOTS_PER_UNIT = {0: 1, 1: 2}
WEIGHTS_AFTER = {0: (0,), 1: (1, 2), 2: (3,)}
TAIL_PIECE = 128


def tile_mix_glubwd_fm_res_kernel(tc, g, u, dh, wg_words, wg_scales, wu_words, wu_scales, r, out):
    nc = tc.nc
    n_chunks = HALVES * PASSES
    units = []
    for c in range(n_chunks):
        step = SLOTS_PER_UNIT.get(c, PACK)
        units.extend([(c, j, j + step) for j in range(0, PACK, step)])
    last = len(units) - 1

    with ExitStack() as ctx:
        raw = ctx.enter_context(tc.tile_pool(name="raw", bufs=4))
        actp = ctx.enter_context(tc.tile_pool(name="actp", bufs=2))
        grp = ctx.enter_context(tc.tile_pool(name="grp", bufs=2))
        codep = ctx.enter_context(tc.tile_pool(name="codep", bufs=4))
        keep = ctx.enter_context(tc.tile_pool(name="keep", bufs=1))
        psum = ctx.enter_context(tc.psum_pool(name="psum", bufs=1))
        ctx.enter_context(tc.manual_schedule())

        wg_plane = keep.tile([P, PASSES, D], U8, name="wg_plane", align_bytes=64)
        wu_plane = keep.tile([P, PASSES, D], U8, name="wu_plane", align_bytes=64)
        for plane, scales in ((wu_plane, wu_scales), (wg_plane, wg_scales)):
            nc.vector.memset(plane[:].bitcast(U32), 0)
            rows = scales.rearrange("a (q s) n -> s q a n", s=4)
            for s in range(4):
                nc.gpsimd.dma_start(out=plane[s:P:32, :, :].bitcast(I32), in_=rows[s].bitcast(I32))

        srcs = {"g": g, "dh": dh, "u": u}
        rawt, st, wts, codes, banks, res, bf = {}, {}, {}, {}, {}, {}, {}

        def load_chunk(c):
            half, a = divmod(c, PASSES)
            for name in srcs:
                rawt[c, name] = raw.tile([P, PACK, N_TILE], F32, name=name, tag=name, bufs=3 if name == "dh" else 4)
            for cc, j0, j1 in units:
                if cc == c:
                    for name in srcs:
                        if c == EPILOGUE_CHUNK and name == "u":
                            load_res(0)
                        rows = srcs[name][a * K_PASS : (a + 1) * K_PASS, half * N_TILE : (half + 1) * N_TILE]
                        nc.sync.dma_start(out=rawt[c, name][:, j0:j1, :], in_=rows.rearrange("(p j) t -> p j t", j=PACK)[:, j0:j1, :])

        def load_weights(a):
            wu_t = keep.tile([P, D], U32, name="wu%d" % a, align_bytes=64)
            nc.sync.dma_start(out=wu_t[:].bitcast(I32), in_=wu_words[a].rearrange("p n i -> p (n i)").bitcast(I32))
            wg_t = keep.tile([P, 2 * D], U8, name="wg%d" % a, align_bytes=64)
            nc.sync.dma_start(out=wg_t[:].bitcast(I32), in_=wg_words[a].bitcast(I32))
            wts[a] = (wg_t, wu_t)

        def load_res(half):
            res[half] = keep.tile([P, M_TILES, N_TILE], F32, name="res%d" % half)
            nc.sync.dma_start(out=res[half][:], in_=r[:, half * N_TILE : (half + 1) * N_TILE].rearrange("(m p) t -> p m t", p=P))

        def part(n, name):
            c, j0, j1 = units[n]
            return rawt[c, name][:, j0:j1, :]

        def scratch(n, name):
            c, j0, j1 = units[n]
            st[n, name] = actp.tile([P, j1 - j0, N_TILE], F32, name=name, tag=name)
            return st[n, name][:]

        def make_th(n):
            nc.scalar.activation(out=scratch(n, "th"), in_=part(n, "g"), func=ACT.Tanh, scale=0.5)

        def make_mneg(n):
            nc.scalar.activation(out=scratch(n, "mneg"), in_=part(n, "g"), func=ACT.Silu, scale=-1.0)

        def make_p(n):
            th = st[n, "th"][:]
            nc.vector.scalar_tensor_tensor(out=th, in0=th, scalar=1.0, in1=part(n, "dh"), op0=ALU.add, op1=ALU.mult)

        def make_du(n, engine):
            engine.tensor_tensor(out=part(n, "g"), in0=st[n, "th"][:], in1=part(n, "g"), op=ALU.mult)

        def make_w(n):
            m = st[n, "mneg"][:]
            nc.vector.scalar_tensor_tensor(out=m, in0=m, scalar=1.0, in1=part(n, "u"), op0=ALU.subtract, op1=ALU.mult)

        def make_dg(n):
            nc.vector.tensor_tensor(out=part(n, "u"), in0=st[n, "th"][:], in1=st[n, "mneg"][:], op=ALU.mult)

        def round_interleave(name, src, dst):
            nc.scalar.activation(
                out=dst.rearrange("p (c i j) -> p c j i", i=2, j=PACK),
                in_=src.rearrange("p j (c i) -> p c j i", i=2),
                func=ACT.Copy,
                scale=0.5 if name == "du" else -0.5,
            )

        def copy_du(c):
            bf[c] = grp.tile([P, 2 * PACK * N_TILE], BF16, name="bf", tag="bf", align_bytes=64)
            round_interleave("du", rawt[c, "g"][:], bf[c][:, : PACK * N_TILE])

        def copy_dg(c):
            round_interleave("dg", rawt[c, "u"][:], bf[c][:, PACK * N_TILE :])

        def quantize(c, first, src):
            if first == 0:
                cw = codep.tile([P, 2 * N_TILE], U32, name="codes", tag="codes", align_bytes=64)
                cs = codep.tile([P, 2 * N_TILE], U8, name="scales", tag="scales", align_bytes=64)
                codes[c] = (cw, cs)
            cw, cs = codes[c]
            cols = slice(first, first + src.shape[1] // PACK)
            nc.vector.quantize_mx(out=cw[:, cols].bitcast(E5M2), scales=cs[:, cols], in_=src)

        def multiply(c, name, m):
            half, a = divmod(c, PASSES)
            cw, cs = codes[c]
            words = slice(0, N_TILE) if name == "du" else slice(N_TILE, 2 * N_TILE)
            wg_t, wu_t = wts[a]
            first = a == 0 and name == "du"
            if first:
                banks[half, m] = psum.tile([P, N_TILE], F32, name="bank%d" % m, tag="bank%d" % m)
            cols = slice(m * P, (m + 1) * P)
            if name == "du":
                lhs, lhs_scale = wu_t[:, cols].bitcast(E4M3), wu_plane[:, a, cols]
            else:
                lhs, lhs_scale = wg_t[:, 2 * m * P : 2 * (m + 1) * P].bitcast(E2M1), wg_plane[:, a, cols]
            nc.tensor.matmul_mx(
                out=banks[half, m][:], lhsT=lhs, lhsT_scale=lhs_scale, rhs=cw[:, words].bitcast(E5M2), rhs_scale=cs[:, words],
                start=first, stop=(a == PASSES - 1 and name == "dg"),
            )

        def multiply_all(c, names):
            for name in names:
                for m in range(M_TILES):
                    multiply(c, name, m)

        def add_residual(half, m):
            t = res[half][:, m, :]
            nc.vector.tensor_tensor(out=t, in0=banks[half, m][:], in1=t, op=ALU.add)

        def store(half, m0, m1):
            dst = out[m0 * P : m1 * P, half * N_TILE : (half + 1) * N_TILE].rearrange("(m p) t -> p m t", p=P)
            nc.sync.dma_start(out=dst, in_=res[half][:, m0:m1, :])

        both = ("du", "dg")
        for c in range(3):
            load_chunk(c)
        make_mneg(0)
        make_th(0)
        for n in range(last):
            c, j0, j1 = units[n]
            if c == 2:
                quantize(0, 0, bf[0][:])
                multiply_all(0, both)
            make_p(n)
            make_th(n + 1)
            if c == EPILOGUE_CHUNK:
                make_du(n, nc.gpsimd)
                for m in range(M_TILES):
                    add_residual(0, m)
                multiply_all(PASSES, both)
                store(0, 0, 4)
                store(0, 4, 8)
            make_w(n)
            make_mneg(n + 1)
            if c == 1 and j0 == 0:
                copy_du(0)
                copy_dg(0)
            if c != EPILOGUE_CHUNK:
                make_du(n, nc.vector)
            if c > 1:
                quantize(c - 1, 0, bf[c - 1][:])
            if j1 == PACK and c > 0:
                copy_du(c)
            make_dg(n)
            if j1 < PACK:
                continue
            if c > 0:
                copy_dg(c)
            for a in WEIGHTS_AFTER.get(c, ()):
                load_weights(a)
            if 2 <= c <= PASSES:
                multiply_all(c - 1, both)
            if c == EPILOGUE_CHUNK:
                multiply_all(c - 1, both)
            if c + 3 < n_chunks:
                load_chunk(c + 3)
            if c + 3 == n_chunks - 1:
                load_res(1)

        c = n_chunks - 1
        make_p(last)
        quantize(c - 1, 0, bf[c - 1][:, : PACK * N_TILE])
        multiply_all(c - 1, ("du",))
        make_du(last, nc.vector)
        copy_du(c)
        quantize(c - 1, N_TILE, bf[c - 1][:, PACK * N_TILE :])
        multiply_all(c - 1, ("dg",))
        make_w(last)
        quantize(c, 0, bf[c][:, : PACK * N_TILE])
        multiply_all(c, ("du",))
        pieces = []
        for i in range(N_TILE // TAIL_PIECE):
            cols = slice(i * TAIL_PIECE, (i + 1) * TAIL_PIECE)
            piece = keep.tile([P, PACK, TAIL_PIECE], F32, name="piece%d" % i)
            nc.vector.tensor_tensor(out=piece[:], in0=st[last, "th"][:, :, cols], in1=st[last, "mneg"][:, :, cols], op=ALU.mult)
            piece_bf = keep.tile([P, PACK * TAIL_PIECE], BF16, name="piece_bf%d" % i, align_bytes=64)
            round_interleave("dg", piece[:], piece_bf[:])
            pieces.append(piece_bf)
        for i, piece_bf in enumerate(pieces):
            quantize(c, N_TILE + i * TAIL_PIECE, piece_bf[:])
        multiply_all(c, ("dg",))
        for m in range(M_TILES):
            add_residual(1, m)
            store(1, m, m + 1)
